import numpy as np
import ml_dtypes


def mxq(x, axis, fmt="e4m3"):
    dtype, down = {"e4m3": (ml_dtypes.float8_e4m3fn, 7), "e5m2": (ml_dtypes.float8_e5m2, 14)}[fmt]
    v = np.moveaxis(np.asarray(x, np.float32).astype(ml_dtypes.bfloat16).astype(np.float64), axis, -1)
    blocks = v.reshape(v.shape[:-1] + (-1, 32))
    amax = np.abs(blocks).max(-1, keepdims=True)
    byte = np.maximum(np.where(amax > 0, np.frexp(amax)[1] - 1 + 127, 0) - down, 1)
    scale = np.exp2(byte - 127.0)
    codes = (blocks / scale).astype(np.float32).astype(dtype).astype(np.float64)
    return np.moveaxis((codes * scale).reshape(v.shape), -1, axis)


WIDE = False


def mx_kscale(k):
    if not WIDE:
        return np.ones(k)
    levels = np.array([10, -10, 5, -5, 0])
    if k % 512:
        return np.exp2(np.random.permutation(np.resize(levels, k // 32))).repeat(32)
    a = np.empty((k // 512, 16))
    for p in range(k // 512):
        a[p, :8] = np.random.permutation(np.resize(levels, 8))
        for g in range(8):
            far = levels[np.abs(levels - a[p, g]) >= 10]
            a[p, g + 8] = far[np.random.randint(len(far))]
    return np.exp2(a.ravel()).repeat(32)


def f64(x):
    return np.asarray(x).astype(np.float64)


E2M1 = np.array([0.0, 0.5, 1.0, 1.5, 2.0, 3.0, 4.0, 6.0, -0.0, -0.5, -1.0, -1.5, -2.0, -3.0, -4.0, -6.0])


def pack_weight(w, fmt):
    k, n = w.shape
    w = f64(np.asarray(w, np.float32).astype(ml_dtypes.bfloat16)).reshape(k // 32, 32, n)
    amax = np.abs(w).max(1)
    if fmt == "e4m3":
        byte = np.frexp(amax)[1] - 1 + 127 - 7
    else:
        mant, ex = np.frexp(amax / 6.0)
        byte = np.where(mant > 0.5, ex, ex - 1) + 127
    byte = np.clip(np.where(amax > 0, byte, 1), 1, 254)
    scaled = (w * np.exp2(127.0 - byte)[:, None, :]).reshape(k, n).astype(np.float32)
    by_word = np.ascontiguousarray(scaled.reshape(k // 512, 128, 4, n).transpose(0, 1, 3, 2))
    if fmt == "e4m3":
        words = by_word.astype(ml_dtypes.float8_e4m3fn).view(np.uint8)
    else:
        c = by_word.astype(ml_dtypes.float4_e2m1fn).view(np.uint8) & 0xF
        words = (c[..., 0::2] | (c[..., 1::2] << 4)).reshape(k // 512, 128, 2 * n)
    return np.ascontiguousarray(words), np.ascontiguousarray(byte.astype(np.uint8).reshape(k // 512, 16, n))


def unpack_weight(words, scales, fmt):
    g, _, n = scales.shape
    words = np.ascontiguousarray(words).reshape(g, 128, n, -1)
    if fmt == "e4m3":
        vals = words.view(ml_dtypes.float8_e4m3fn).astype(np.float64)
    else:
        nib = np.empty((g, 128, n, 4), np.uint8)
        nib[..., 0::2] = words & 0xF
        nib[..., 1::2] = words >> 4
        vals = E2M1[nib]
    vals = vals * np.repeat(np.exp2(scales.astype(np.float64) - 127.0), 8, axis=1)[..., None]
    return vals.transpose(0, 1, 3, 2).reshape(g * 512, n)


K, L, T, R, N = 1024, 512, 512, 512, 512


def setup_inputs():
    n = np.random.standard_normal
    fk = mx_kscale(K)
    fl = mx_kscale(L)
    fr = mx_kscale(R)
    xtp = pack_weight(n((K, T)) / fk[:, None], "e4m3")
    wap = pack_weight(n((K, R)) * 1 / np.sqrt(K) * fk[:, None], "e2m1")
    xqp = pack_weight(n((L, T)) / fl[:, None], "e4m3")
    wcp = pack_weight(n((L, R)) * 1 / np.sqrt(L) * fl[:, None], "e2m1")
    wbp = pack_weight(n((R, N)) * 1 / np.sqrt(R) / fr[:, None], "e4m3")
    wyp = pack_weight(n((K, N)) * 1 / np.sqrt(K) * fk[:, None], "e2m1")
    return {
        "xt_words": xtp[0],
        "xt_scales": xtp[1],
        "wa_words": wap[0],
        "wa_scales": wap[1],
        "xq_words": xqp[0],
        "xq_scales": xqp[1],
        "wc_words": wcp[0],
        "wc_scales": wcp[1],
        "us": (np.random.uniform(0.5, 2.0, (R, 1)) * fr[:, None]).astype(np.float32),
        "wb_words": wbp[0],
        "wb_scales": wbp[1],
        "wy_words": wyp[0],
        "wy_scales": wyp[1],
    }


def reference(xt_words, xt_scales, wa_words, wa_scales, xq_words, xq_scales, wc_words, wc_scales, us, wb_words, wb_scales, wy_words, wy_scales):
    xtu = unpack_weight(xt_words, xt_scales, "e4m3")
    wau = unpack_weight(wa_words, wa_scales, "e2m1")
    xqu = unpack_weight(xq_words, xq_scales, "e4m3")
    wcu = unpack_weight(wc_words, wc_scales, "e2m1")
    wbu = unpack_weight(wb_words, wb_scales, "e4m3")
    wyu = unpack_weight(wy_words, wy_scales, "e2m1")
    a = wau.T @ xtu
    b = wcu.T @ xqu
    hid = a / (1.0 + np.abs(b)) * f64(us)
    hidq = mxq(hid, 0, "e4m3")
    y = wbu.T @ hidq + wyu.T @ xtu
    return y

@@ -1,0 +1,244 @@
+from contextlib import ExitStack
+
+import concourse.mybir as mybir
+
+K, L, T, R, N = 1024, 512, 512, 512, 512
+FLOPS = 2 * T * (K * R + L * R + R * N + K * N)
+
+F32 = mybir.dt.float32
+BF16 = mybir.dt.bfloat16
+I32 = mybir.dt.int32
+U32 = mybir.dt.uint32
+U16 = mybir.dt.uint16
+U8 = mybir.dt.uint8
+FP8X4 = mybir.dt.float8_e4m3fn_x4
+FP4X4 = mybir.dt.float4_e2m1fn_x4
+ACT = mybir.ActivationFunctionType
+ALU = mybir.AluOpType
+
+P = 128
+PACK = 4
+CH = 128
+NCH = T // CH
+
+
+def tile_mix_hidden_divided_hidden_kernel(
+    tc, xt_words, xt_scales, wa_words, wa_scales, xq_words, xq_scales, wc_words, wc_scales,
+    us, wb_words, wb_scales, wy_words, wy_scales, out,
+):
+    nc = tc.nc
+    with ExitStack() as ctx:
+        keep = ctx.enter_context(tc.tile_pool(name="keep", bufs=1))
+        psum = ctx.enter_context(tc.psum_pool(name="psum", bufs=1))
+        ctx.enter_context(tc.manual_schedule())
+
+        def sb(name, shape, dtype):
+            return keep.tile(shape, dtype, name=name, align_bytes=64)
+
+        xt_w = sb("xt_w", [P, 2, T], U32)
+        xq_w = sb("xq_w", [P, 1, T], U32)
+        wb_w = sb("wb_w", [P, 1, N], U32)
+        wy_w = sb("wy_w", [P, 2, 2 * N], U8)
+        wa_raw = sb("wa_raw", [P, 2, 2 * R], U8)
+        wc_raw = sb("wc_raw", [P, 1, 2 * R], U8)
+        wa_w = sb("wa_w", [P, PACK, 2, 2 * P], U8)
+        wc_w = sb("wc_w", [P, PACK, 1, 2 * P], U8)
+        wa_s = sb("wa_s", [P, PACK, 2, P], U8)
+        wc_s = sb("wc_s", [P, PACK, 1, P], U8)
+        first_planes = sb("first_planes", [P, 2 * 512], U8)
+        second_planes = sb("second_planes", [P, 4 * 512], U8)
+        third_planes = sb("third_planes", [P, 3 * 512], U8)
+        wc_sraw = first_planes[:, 0:512]
+        xq_s = first_planes[:, 512:1024]
+        wa_sraw = second_planes[:, 0:1024]
+        xt_s = second_planes[:, 1024:2048]
+        wy_s = third_planes[:, 0:1024]
+        wb_s = third_planes[:, 1024:1536]
+        us_sb = sb("us_sb", [P, PACK], F32)
+
+        def load_e4m3(eng, tile, words):
+            eng.dma_start(out=tile[:].bitcast(I32), in_=words.rearrange("z p c r -> p z (c r)").bitcast(I32))
+
+        def load_e2m1(eng, tile, words):
+            eng.dma_start(out=tile[:].bitcast(I32), in_=words.rearrange("z p c -> p z c").bitcast(I32))
+
+        def load_scale_rows(eng, planes, lo, scales, r):
+            z = scales.shape[0]
+            dst = planes[r:P:32, lo:lo + 512 * z].bitcast(I32).rearrange("q (z c) -> q z c", z=z)
+            src = scales.rearrange("z (q r) c -> r q z c", r=4)[r].bitcast(I32)
+            eng.dma_start(out=dst, in_=src)
+
+        nc.vector.memset(first_planes[:].bitcast(I32), 0)
+        nc.vector.memset(second_planes[:].bitcast(I32), 0)
+        nc.vector.memset(third_planes[:].bitcast(I32), 0)
+
+        load_e2m1(nc.sync, wc_raw, wc_words)
+        load_e4m3(nc.scalar, xq_w, xq_words)
+        load_e2m1(nc.sync, wa_raw, wa_words)
+        nc.gpsimd.dma_start(out=us_sb[:], in_=us.rearrange("(p j) o -> p (j o)", j=PACK))
+        for r in range(4):
+            load_scale_rows(nc.sync, first_planes, 0, wc_scales, r)
+        for r in range(4):
+            load_scale_rows(nc.sync, first_planes, 512, xq_scales, r)
+        for r in range(2):
+            load_scale_rows(nc.gpsimd, second_planes, 1024, xt_scales, r)
+        for r in range(4):
+            load_scale_rows(nc.sync, second_planes, 0, wa_scales, r)
+        load_e4m3(nc.sync, xt_w, xt_words)
+        for r in range(2, 4):
+            load_scale_rows(nc.sync, second_planes, 1024, xt_scales, r)
+        load_e2m1(nc.sync, wy_w, wy_words)
+        for r in range(4):
+            load_scale_rows(nc.sync, third_planes, 0, wy_scales, r)
+        load_e4m3(nc.sync, wb_w, wb_words)
+        for r in range(4):
+            load_scale_rows(nc.sync, third_planes, 1024, wb_scales, r)
+
+        warm = sb("warm", [P, 2], F32)
+        nc.vector.memset(warm[:], 1.0)
+        nc.scalar.activation(out=warm[:, 1:2], in_=warm[:, 0:1], func=ACT.Abs_reciprocal_sqrt)
+
+        nc.scalar.copy(
+            out=wc_w[:].rearrange("p j z b -> p j (z b)").bitcast(U16).rearrange("p j (g i) -> p g j i", i=8),
+            in_=wc_raw[:].rearrange("p z b -> p (z b)").bitcast(U16).rearrange("p (g i j) -> p g j i", i=8, j=PACK),
+        )
+        nc.vector.tensor_copy(
+            out=wc_s[:].rearrange("p j z (g i) -> p (z g) j i", i=16),
+            in_=wc_sraw.rearrange("p (g i j) -> p g j i", i=16, j=PACK),
+        )
+        nc.vector.tensor_copy(
+            out=wa_w[:].rearrange("p j z b -> p j (z b)").bitcast(U16).rearrange("p j (g i) -> p g j i", i=8),
+            in_=wa_raw[:].rearrange("p z b -> p (z b)").bitcast(U16).rearrange("p (g i j) -> p g j i", i=8, j=PACK),
+        )
+        nc.vector.tensor_copy(
+            out=wa_s[:].rearrange("p j z (g i) -> p (z g) j i", i=16),
+            in_=wa_sraw.rearrange("p (g i j) -> p g j i", i=16, j=PACK),
+        )
+
+        b_banks, a_banks, o_banks = {}, {}, {}
+        q_t, w_t, hid_t, hq_w, hq_s = {}, {}, {}, {}, {}
+
+        def tok(c):
+            return slice(c * CH, (c + 1) * CH)
+
+        def mm_b(c):
+            bank = psum.tile([P, PACK, CH], F32, name="b_bank", tag="bank%d" % c)
+            b_banks[c] = bank
+            for j in range(PACK):
+                nc.tensor.matmul_mx(
+                    out=bank[:, j, :], lhsT=wc_w[:, j, 0, :].bitcast(FP4X4), lhsT_scale=wc_s[:, j, 0, :],
+                    rhs=xq_w[:, 0, tok(c)].bitcast(FP8X4), rhs_scale=xq_s[:, tok(c)], start=True, stop=True)
+
+        def mm_a(c):
+            bank = psum.tile([P, PACK, CH], F32, name="a_bank", tag="bank%d" % (NCH + c))
+            a_banks[c] = bank
+            for j in range(PACK):
+                for z in range(2):
+                    nc.tensor.matmul_mx(
+                        out=bank[:, j, :], lhsT=wa_w[:, j, z, :].bitcast(FP4X4), lhsT_scale=wa_s[:, j, z, :],
+                        rhs=xt_w[:, z, tok(c)].bitcast(FP8X4),
+                        rhs_scale=xt_s[:, 512 * z + c * CH:512 * z + (c + 1) * CH], start=(z == 0), stop=(z == 1))
+
+        def mm_y(c):
+            if c < NCH - 1:
+                bank = psum.tile([P, N // P, CH], F32, name="o_bank", tag="bank%d" % c)
+                o_banks[c] = [(bank, 0, 4)]
+            else:
+                lo = psum.tile([P, 2, CH], F32, name="o_lo", tag="bank%d" % c)
+                hi = psum.tile([P, 2, CH], F32, name="o_hi", tag="bank%d" % NCH)
+                o_banks[c] = [(lo, 0, 2), (hi, 2, 4)]
+            for bank, a0, a1 in o_banks[c]:
+                for a in range(a0, a1):
+                    for z in range(2):
+                        nc.tensor.matmul_mx(
+                            out=bank[:, a - a0, :], lhsT=wy_w[:, z, 2 * P * a:2 * P * (a + 1)].bitcast(FP4X4),
+                            lhsT_scale=wy_s[:, 512 * z + P * a:512 * z + P * (a + 1)],
+                            rhs=xt_w[:, z, tok(c)].bitcast(FP8X4),
+                            rhs_scale=xt_s[:, 512 * z + c * CH:512 * z + (c + 1) * CH],
+                            start=(a == a0 and z == 0), stop=False)
+
+        def mm_o(c):
+            for bank, a0, a1 in o_banks[c]:
+                for a in range(a0, a1):
+                    nc.tensor.matmul_mx(
+                        out=bank[:, a - a0, :], lhsT=wb_w[:, 0, P * a:P * (a + 1)].bitcast(FP8X4),
+                        lhsT_scale=wb_s[:, P * a:P * (a + 1)],
+                        rhs=hq_w[c][:].bitcast(FP8X4), rhs_scale=hq_s[c][:], start=False, stop=(a == a1 - 1))
+
+        def root(c):
+            halves = (slice(0, 2), slice(2, 4))
+            d = keep.tile([P, PACK, CH], F32, name="absb", bufs=2)
+            for h in halves:
+                nc.scalar.activation(out=d[:, h, :], in_=b_banks[c][:, h, :], func=ACT.Abs)
+            q = keep.tile([P, PACK, CH], F32, name="q", bufs=NCH)
+            for h in halves:
+                nc.scalar.activation(out=q[:, h, :], in_=d[:, h, :], func=ACT.Abs_reciprocal_sqrt, bias=1.0)
+            q_t[c] = q
+
+        def factor(c):
+            w = keep.tile([P, PACK, CH], F32, name="w", bufs=NCH)
+            for j in range(PACK):
+                nc.vector.scalar_tensor_tensor(
+                    out=w[:, j, :], in0=q_t[c][:, j, :], scalar=us_sb[:, j:j + 1], in1=q_t[c][:, j, :],
+                    op0=ALU.mult, op1=ALU.mult)
+            w_t[c] = w
+
+        def hidden(c):
+            h = keep.tile([P, CH, PACK], BF16, name="hid", bufs=NCH, align_bytes=64)
+            nc.vector.tensor_tensor(
+                out=h[:].rearrange("p (g i) j -> p g j i", i=4),
+                in0=a_banks[c][:].rearrange("p j (g i) -> p g j i", i=4),
+                in1=w_t[c][:].rearrange("p j (g i) -> p g j i", i=4), op=ALU.mult)
+            hid_t[c] = h
+
+        def quant(c):
+            cw = keep.tile([P, CH], U32, name="hq_w", bufs=NCH, align_bytes=64)
+            cs = keep.tile([P, CH], U8, name="hq_s", bufs=NCH, align_bytes=64)
+            nc.vector.quantize_mx(out=cw[:].bitcast(FP8X4), scales=cs[:], in_=hid_t[c][:].rearrange("p t j -> p (t j)"))
+            hq_w[c], hq_s[c] = cw, cs
+
+        out_v = out.rearrange("(a p) t -> p a t", p=P)
+
+        def drain(c):
+            for n, (bank, a0, a1) in enumerate(o_banks[c]):
+                res = keep.tile([P, a1 - a0, CH], F32, name="res", bufs=NCH + 1)
+                if n == 0:
+                    nc.scalar.copy(out=res[:], in_=bank[:])
+                else:
+                    nc.vector.tensor_copy(out=res[:], in_=bank[:])
+                nc.sync.dma_start(out=out_v[:, a0:a1, tok(c)], in_=res[:])
+
+        mm_b(0)
+        mm_b(1)
+        mm_b(2)
+        root(0)
+        root(1)
+        mm_a(0)
+        mm_b(3)
+        mm_a(1)
+        factor(0)
+        hidden(0)
+        root(2)
+        root(3)
+        mm_y(0)
+        mm_a(2)
+        factor(1)
+        quant(0)
+        hidden(1)
+        mm_o(0)
+        mm_a(3)
+        mm_y(1)
+        factor(2)
+        quant(1)
+        hidden(2)
+        mm_o(1)
+        mm_y(2)
+        mm_y(3)
+        factor(3)
+        quant(2)
+        hidden(3)
+        quant(3)
+        mm_o(2)
+        mm_o(3)
+        for c in range(NCH):
+            drain(c)

@@ -35,7 +35,11 @@ def tile_mix_hidden_divided_hidden_kernel(
         def sb(name, shape, dtype):
             return keep.tile(shape, dtype, name=name, align_bytes=64)
 
-        xt_w = sb("xt_w", [P, 2, T], U32)
+        xt_h = [sb("xt_w%d" % h, [P, 2, 256], U32) for h in range(2)]
+
+        def xt_codes(z, t0, nt):
+            return xt_h[t0 // 256][:, z, t0 % 256:t0 % 256 + nt].bitcast(FP8X4)
+
         xq_w = sb("xq_w", [P, 1, T], U32)
         wb_w = sb("wb_w", [P, 1, N], U32)
         wy_w = sb("wy_w", [P, 2, 2 * N], U8)
@@ -68,25 +72,30 @@ def tile_mix_hidden_divided_hidden_kernel(
             src = scales.rearrange("z (q r) c -> r q z c", r=4)[r].bitcast(I32)
             eng.dma_start(out=dst, in_=src)
 
-        nc.vector.memset(first_planes[:].bitcast(I32), 0)
-        nc.vector.memset(second_planes[:].bitcast(I32), 0)
+        nc.gpsimd.memset(wc_sraw.bitcast(I32), 0)
+        nc.vector.memset(xq_s.bitcast(I32), 0)
+        nc.vector.memset(xt_s.bitcast(I32), 0)
+        nc.vector.memset(wa_sraw.bitcast(I32), 0)
         nc.vector.memset(third_planes[:].bitcast(I32), 0)
 
-        load_e2m1(nc.sync, wc_raw, wc_words)
-        load_e4m3(nc.scalar, xq_w, xq_words)
-        load_e2m1(nc.sync, wa_raw, wa_words)
-        nc.gpsimd.dma_start(out=us_sb[:], in_=us.rearrange("(p j) o -> p (j o)", j=PACK))
+        xt_v = xt_words.rearrange("z p c r -> p z (c r)").bitcast(I32)
+
         for r in range(4):
             load_scale_rows(nc.sync, first_planes, 0, wc_scales, r)
+        load_e2m1(nc.sync, wc_raw, wc_words)
+        load_e4m3(nc.sync, xq_w, xq_words)
         for r in range(4):
             load_scale_rows(nc.sync, first_planes, 512, xq_scales, r)
+        nc.gpsimd.dma_start(out=us_sb[:], in_=us.rearrange("(p j) o -> p (j o)", j=PACK))
         for r in range(2):
-            load_scale_rows(nc.gpsimd, second_planes, 1024, xt_scales, r)
-        for r in range(4):
             load_scale_rows(nc.sync, second_planes, 0, wa_scales, r)
-        load_e4m3(nc.sync, xt_w, xt_words)
+        load_e2m1(nc.sync, wa_raw, wa_words)
         for r in range(2, 4):
+            load_scale_rows(nc.sync, second_planes, 0, wa_scales, r)
+        nc.sync.dma_start(out=xt_h[0][:].bitcast(I32), in_=xt_v[:, :, 0:256])
+        for r in range(4):
             load_scale_rows(nc.sync, second_planes, 1024, xt_scales, r)
+        nc.sync.dma_start(out=xt_h[1][:].bitcast(I32), in_=xt_v[:, :, 256:512])
         load_e2m1(nc.sync, wy_w, wy_words)
         for r in range(4):
             load_scale_rows(nc.sync, third_planes, 0, wy_scales, r)
@@ -110,13 +119,14 @@ def tile_mix_hidden_divided_hidden_kernel(
             out=wa_w[:].rearrange("p j z b -> p j (z b)").bitcast(U16).rearrange("p j (g i) -> p g j i", i=8),
             in_=wa_raw[:].rearrange("p z b -> p (z b)").bitcast(U16).rearrange("p (g i j) -> p g j i", i=8, j=PACK),
         )
-        nc.vector.tensor_copy(
-            out=wa_s[:].rearrange("p j z (g i) -> p (z g) j i", i=16),
-            in_=wa_sraw.rearrange("p (g i j) -> p g j i", i=16, j=PACK),
-        )
+        for h in (slice(0, 2), slice(2, 4)):
+            nc.vector.tensor_copy(
+                out=wa_s[:, h, :, :].rearrange("p j z (g i) -> p (z g) j i", i=16),
+                in_=wa_sraw.rearrange("p (g i j) -> p g j i", i=16, j=PACK)[:, :, h, :],
+            )
 
         b_banks, a_banks, o_banks = {}, {}, {}
-        q_t, w_t, hid_t, hq_w, hq_s = {}, {}, {}, {}, {}
+        q_t, w_t, hq_w, hq_s = {}, {}, {}, {}
 
         def tok(c):
             return slice(c * CH, (c + 1) * CH)
@@ -136,34 +146,37 @@ def tile_mix_hidden_divided_hidden_kernel(
                 for z in range(2):
                     nc.tensor.matmul_mx(
                         out=bank[:, j, :], lhsT=wa_w[:, j, z, :].bitcast(FP4X4), lhsT_scale=wa_s[:, j, z, :],
-                        rhs=xt_w[:, z, tok(c)].bitcast(FP8X4),
+                        rhs=xt_codes(z, c * CH, CH),
                         rhs_scale=xt_s[:, 512 * z + c * CH:512 * z + (c + 1) * CH], start=(z == 0), stop=(z == 1))
 
-        def mm_y(c):
-            if c < NCH - 1:
-                bank = psum.tile([P, N // P, CH], F32, name="o_bank", tag="bank%d" % c)
-                o_banks[c] = [(bank, 0, 4)]
-            else:
-                lo = psum.tile([P, 2, CH], F32, name="o_lo", tag="bank%d" % c)
-                hi = psum.tile([P, 2, CH], F32, name="o_hi", tag="bank%d" % NCH)
-                o_banks[c] = [(lo, 0, 2), (hi, 2, 4)]
-            for bank, a0, a1 in o_banks[c]:
-                for a in range(a0, a1):
-                    for z in range(2):
-                        nc.tensor.matmul_mx(
-                            out=bank[:, a - a0, :], lhsT=wy_w[:, z, 2 * P * a:2 * P * (a + 1)].bitcast(FP4X4),
-                            lhsT_scale=wy_s[:, 512 * z + P * a:512 * z + P * (a + 1)],
-                            rhs=xt_w[:, z, tok(c)].bitcast(FP8X4),
-                            rhs_scale=xt_s[:, 512 * z + c * CH:512 * z + (c + 1) * CH],
-                            start=(a == a0 and z == 0), stop=False)
+        groups = [
+            (0, 256, [(0, 0, 2), (1, 2, 4)]),
+            (256, 128, [(2, 0, 4)]),
+            (384, 128, [(3, 0, 2), (4, 2, 4)]),
+        ]
 
-        def mm_o(c):
-            for bank, a0, a1 in o_banks[c]:
-                for a in range(a0, a1):
+        def mm_y(g, part):
+            t0, nt, parts = groups[g]
+            tag, a0, a1 = parts[part]
+            bank = psum.tile([P, a1 - a0, nt], F32, name="o_bank", tag="bank%d" % tag)
+            o_banks[g, part] = bank
+            for a in range(a0, a1):
+                for z in range(2):
                     nc.tensor.matmul_mx(
-                        out=bank[:, a - a0, :], lhsT=wb_w[:, 0, P * a:P * (a + 1)].bitcast(FP8X4),
-                        lhsT_scale=wb_s[:, P * a:P * (a + 1)],
-                        rhs=hq_w[c][:].bitcast(FP8X4), rhs_scale=hq_s[c][:], start=False, stop=(a == a1 - 1))
+                        out=bank[:, a - a0, :], lhsT=wy_w[:, z, 2 * P * a:2 * P * (a + 1)].bitcast(FP4X4),
+                        lhsT_scale=wy_s[:, 512 * z + P * a:512 * z + P * (a + 1)],
+                        rhs=xt_codes(z, t0, nt),
+                        rhs_scale=xt_s[:, 512 * z + t0:512 * z + t0 + nt],
+                        start=(a == a0 and z == 0), stop=False)
+
+        def mm_o(g, part):
+            t0, nt, parts = groups[g]
+            tag, a0, a1 = parts[part]
+            for a in range(a0, a1):
+                nc.tensor.matmul_mx(
+                    out=o_banks[g, part][:, a - a0, :], lhsT=wb_w[:, 0, P * a:P * (a + 1)].bitcast(FP8X4),
+                    lhsT_scale=wb_s[:, P * a:P * (a + 1)],
+                    rhs=hq_w[g][:].bitcast(FP8X4), rhs_scale=hq_s[g][:], start=False, stop=(a == a1 - 1))
 
         def root(c):
             halves = (slice(0, 2), slice(2, 4))
@@ -183,62 +196,61 @@ def tile_mix_hidden_divided_hidden_kernel(
                     op0=ALU.mult, op1=ALU.mult)
             w_t[c] = w
 
+        hid = sb("hid", [P, T * PACK], BF16)
+
         def hidden(c):
-            h = keep.tile([P, CH, PACK], BF16, name="hid", bufs=NCH, align_bytes=64)
             nc.vector.tensor_tensor(
-                out=h[:].rearrange("p (g i) j -> p g j i", i=4),
+                out=hid[:, c * CH * PACK:(c + 1) * CH * PACK].rearrange("p (g i j) -> p g j i", i=4, j=PACK),
                 in0=a_banks[c][:].rearrange("p j (g i) -> p g j i", i=4),
                 in1=w_t[c][:].rearrange("p j (g i) -> p g j i", i=4), op=ALU.mult)
-            hid_t[c] = h
 
-        def quant(c):
-            cw = keep.tile([P, CH], U32, name="hq_w", bufs=NCH, align_bytes=64)
-            cs = keep.tile([P, CH], U8, name="hq_s", bufs=NCH, align_bytes=64)
-            nc.vector.quantize_mx(out=cw[:].bitcast(FP8X4), scales=cs[:], in_=hid_t[c][:].rearrange("p t j -> p (t j)"))
-            hq_w[c], hq_s[c] = cw, cs
+        def quant(g):
+            t0, nt, parts = groups[g]
+            cw = sb("hq_w%d" % g, [P, nt], U32)
+            cs = sb("hq_s%d" % g, [P, nt], U8)
+            nc.vector.quantize_mx(out=cw[:].bitcast(FP8X4), scales=cs[:], in_=hid[:, t0 * PACK:(t0 + nt) * PACK])
+            hq_w[g], hq_s[g] = cw, cs
 
         out_v = out.rearrange("(a p) t -> p a t", p=P)
 
-        def drain(c):
-            for n, (bank, a0, a1) in enumerate(o_banks[c]):
-                res = keep.tile([P, a1 - a0, CH], F32, name="res", bufs=NCH + 1)
-                if n == 0:
-                    nc.scalar.copy(out=res[:], in_=bank[:])
-                else:
-                    nc.vector.tensor_copy(out=res[:], in_=bank[:])
-                nc.sync.dma_start(out=out_v[:, a0:a1, tok(c)], in_=res[:])
+        def drain(g, part, on_vector):
+            t0, nt, parts = groups[g]
+            tag, a0, a1 = parts[part]
+            res = keep.tile([P, a1 - a0, nt], F32, name="res", bufs=5)
+            if on_vector:
+                nc.vector.tensor_copy(out=res[:], in_=o_banks[g, part][:])
+            else:
+                nc.scalar.copy(out=res[:], in_=o_banks[g, part][:])
+            nc.sync.dma_start(out=out_v[:, a0:a1, t0:t0 + nt], in_=res[:])
 
-        mm_b(0)
-        mm_b(1)
-        mm_b(2)
-        root(0)
-        root(1)
-        mm_a(0)
-        mm_b(3)
-        mm_a(1)
-        factor(0)
-        hidden(0)
-        root(2)
-        root(3)
-        mm_y(0)
-        mm_a(2)
-        factor(1)
-        quant(0)
-        hidden(1)
-        mm_o(0)
-        mm_a(3)
-        mm_y(1)
-        factor(2)
-        quant(1)
-        hidden(2)
-        mm_o(1)
-        mm_y(2)
-        mm_y(3)
-        factor(3)
-        quant(2)
-        hidden(3)
-        quant(3)
-        mm_o(2)
-        mm_o(3)
         for c in range(NCH):
-            drain(c)
+            mm_b(c)
+            root(c)
+        for c in range(NCH):
+            mm_a(c)
+        factor(0)
+        factor(1)
+        hidden(0)
+        hidden(1)
+        factor(2)
+        quant(0)
+        hidden(2)
+        factor(3)
+        quant(1)
+        hidden(3)
+        quant(2)
+        mm_y(0, 0)
+        mm_y(0, 1)
+        mm_o(0, 0)
+        mm_o(0, 1)
+        mm_y(1, 0)
+        mm_o(1, 0)
+        mm_y(2, 0)
+        mm_y(2, 1)
+        mm_o(2, 0)
+        mm_o(2, 1)
+        drain(0, 0, False)
+        drain(0, 1, False)
+        drain(1, 0, False)
+        drain(2, 0, False)
+        drain(2, 1, True)

@@ -49,15 +49,12 @@ def tile_mix_hidden_divided_hidden_kernel(
         wc_w = sb("wc_w", [P, PACK, 1, 2 * P], U8)
         wa_s = sb("wa_s", [P, PACK, 2, P], U8)
         wc_s = sb("wc_s", [P, PACK, 1, P], U8)
-        first_planes = sb("first_planes", [P, 2 * 512], U8)
-        second_planes = sb("second_planes", [P, 4 * 512], U8)
-        third_planes = sb("third_planes", [P, 3 * 512], U8)
-        wc_sraw = first_planes[:, 0:512]
-        xq_s = first_planes[:, 512:1024]
-        wa_sraw = second_planes[:, 0:1024]
-        xt_s = second_planes[:, 1024:2048]
-        wy_s = third_planes[:, 0:1024]
-        wb_s = third_planes[:, 1024:1536]
+        wc_sraw = sb("wc_sraw", [P, R], U8)
+        xq_s = sb("xq_s", [P, T], U8)
+        wa_sraw = sb("wa_sraw", [P, 2 * R], U8)
+        xt_s = sb("xt_s", [P, 2 * T], U8)
+        wy_s = sb("wy_s", [P, 2 * N], U8)
+        wb_s = sb("wb_s", [P, N], U8)
         us_sb = sb("us_sb", [P, PACK], F32)
 
         def load_e4m3(eng, tile, words):
@@ -66,42 +63,40 @@ def tile_mix_hidden_divided_hidden_kernel(
         def load_e2m1(eng, tile, words):
             eng.dma_start(out=tile[:].bitcast(I32), in_=words.rearrange("z p c -> p z c").bitcast(I32))
 
-        def load_scale_rows(eng, planes, lo, scales, r):
+        def load_scale_rows(eng, plane, scales, r):
             z = scales.shape[0]
-            dst = planes[r:P:32, lo:lo + 512 * z].bitcast(I32).rearrange("q (z c) -> q z c", z=z)
+            dst = plane[r:P:32, :].bitcast(I32).rearrange("q (z c) -> q z c", z=z)
             src = scales.rearrange("z (q r) c -> r q z c", r=4)[r].bitcast(I32)
             eng.dma_start(out=dst, in_=src)
 
-        nc.gpsimd.memset(wc_sraw.bitcast(I32), 0)
-        nc.vector.memset(xq_s.bitcast(I32), 0)
-        nc.vector.memset(xt_s.bitcast(I32), 0)
-        nc.vector.memset(wa_sraw.bitcast(I32), 0)
-        nc.vector.memset(third_planes[:].bitcast(I32), 0)
+        nc.gpsimd.memset(wc_sraw[:].bitcast(I32), 0)
+        for plane in (xq_s, wa_sraw, xt_s, wy_s, wb_s):
+            nc.vector.memset(plane[:].bitcast(I32), 0)
 
         xt_v = xt_words.rearrange("z p c r -> p z (c r)").bitcast(I32)
 
         for r in range(4):
-            load_scale_rows(nc.sync, first_planes, 0, wc_scales, r)
+            load_scale_rows(nc.sync, wc_sraw, wc_scales, r)
         load_e2m1(nc.sync, wc_raw, wc_words)
         load_e4m3(nc.sync, xq_w, xq_words)
         for r in range(4):
-            load_scale_rows(nc.sync, first_planes, 512, xq_scales, r)
+            load_scale_rows(nc.sync, xq_s, xq_scales, r)
         nc.gpsimd.dma_start(out=us_sb[:], in_=us.rearrange("(p j) o -> p (j o)", j=PACK))
         for r in range(2):
-            load_scale_rows(nc.sync, second_planes, 0, wa_scales, r)
+            load_scale_rows(nc.sync, wa_sraw, wa_scales, r)
         load_e2m1(nc.sync, wa_raw, wa_words)
         for r in range(2, 4):
-            load_scale_rows(nc.sync, second_planes, 0, wa_scales, r)
+            load_scale_rows(nc.sync, wa_sraw, wa_scales, r)
         nc.sync.dma_start(out=xt_h[0][:].bitcast(I32), in_=xt_v[:, :, 0:256])
         for r in range(4):
-            load_scale_rows(nc.sync, second_planes, 1024, xt_scales, r)
+            load_scale_rows(nc.sync, xt_s, xt_scales, r)
         nc.sync.dma_start(out=xt_h[1][:].bitcast(I32), in_=xt_v[:, :, 256:512])
         load_e2m1(nc.sync, wy_w, wy_words)
         for r in range(4):
-            load_scale_rows(nc.sync, third_planes, 0, wy_scales, r)
+            load_scale_rows(nc.sync, wy_s, wy_scales, r)
         load_e4m3(nc.sync, wb_w, wb_words)
         for r in range(4):
-            load_scale_rows(nc.sync, third_planes, 1024, wb_scales, r)
+            load_scale_rows(nc.sync, wb_s, wb_scales, r)
 
         warm = sb("warm", [P, 2], F32)
         nc.vector.memset(warm[:], 1.0)
@@ -113,7 +108,7 @@ def tile_mix_hidden_divided_hidden_kernel(
         )
         nc.vector.tensor_copy(
             out=wc_s[:].rearrange("p j z (g i) -> p (z g) j i", i=16),
-            in_=wc_sraw.rearrange("p (g i j) -> p g j i", i=16, j=PACK),
+            in_=wc_sraw[:].rearrange("p (g i j) -> p g j i", i=16, j=PACK),
         )
         nc.vector.tensor_copy(
             out=wa_w[:].rearrange("p j z b -> p j (z b)").bitcast(U16).rearrange("p j (g i) -> p g j i", i=8),
@@ -122,7 +117,7 @@ def tile_mix_hidden_divided_hidden_kernel(
         for h in (slice(0, 2), slice(2, 4)):
             nc.vector.tensor_copy(
                 out=wa_s[:, h, :, :].rearrange("p j z (g i) -> p (z g) j i", i=16),
-                in_=wa_sraw.rearrange("p (g i j) -> p g j i", i=16, j=PACK)[:, :, h, :],
+                in_=wa_sraw[:].rearrange("p (g i j) -> p g j i", i=16, j=PACK)[:, :, h, :],
             )
 
         b_banks, a_banks, o_banks = {}, {}, {}
@@ -131,13 +126,15 @@ def tile_mix_hidden_divided_hidden_kernel(
         def tok(c):
             return slice(c * CH, (c + 1) * CH)
 
-        def mm_b(c):
-            bank = psum.tile([P, PACK, CH], F32, name="b_bank", tag="bank%d" % c)
-            b_banks[c] = bank
-            for j in range(PACK):
+        def mm_b(h, jp):
+            bank = psum.tile([P, 2, 256], F32, name="b_bank", tag="bank%d" % (2 * h + jp))
+            b_banks[h, jp] = bank
+            for jj in range(2):
+                j = 2 * jp + jj
                 nc.tensor.matmul_mx(
-                    out=bank[:, j, :], lhsT=wc_w[:, j, 0, :].bitcast(FP4X4), lhsT_scale=wc_s[:, j, 0, :],
-                    rhs=xq_w[:, 0, tok(c)].bitcast(FP8X4), rhs_scale=xq_s[:, tok(c)], start=True, stop=True)
+                    out=bank[:, jj, :], lhsT=wc_w[:, j, 0, :].bitcast(FP4X4), lhsT_scale=wc_s[:, j, 0, :],
+                    rhs=xq_w[:, 0, 256 * h:256 * (h + 1)].bitcast(FP8X4), rhs_scale=xq_s[:, 256 * h:256 * (h + 1)],
+                    start=True, stop=True)
 
         def mm_a(c):
             bank = psum.tile([P, PACK, CH], F32, name="a_bank", tag="bank%d" % (NCH + c))
@@ -178,15 +175,29 @@ def tile_mix_hidden_divided_hidden_kernel(
                     lhsT_scale=wb_s[:, P * a:P * (a + 1)],
                     rhs=hq_w[g][:].bitcast(FP8X4), rhs_scale=hq_s[g][:], start=False, stop=(a == a1 - 1))
 
-        def root(c):
-            halves = (slice(0, 2), slice(2, 4))
-            d = keep.tile([P, PACK, CH], F32, name="absb", bufs=2)
-            for h in halves:
-                nc.scalar.activation(out=d[:, h, :], in_=b_banks[c][:, h, :], func=ACT.Abs)
-            q = keep.tile([P, PACK, CH], F32, name="q", bufs=NCH)
-            for h in halves:
-                nc.scalar.activation(out=q[:, h, :], in_=d[:, h, :], func=ACT.Abs_reciprocal_sqrt, bias=1.0)
-            q_t[c] = q
+        def root(h):
+            first, second = 2 * h, 2 * h + 1
+            d = {}
+            for c in (first, second):
+                d[c] = keep.tile([P, PACK, CH], F32, name="absb", bufs=2)
+                q_t[c] = keep.tile([P, PACK, CH], F32, name="q", bufs=NCH)
+
+            def magnitude(c, jp):
+                lo = (c % 2) * CH
+                nc.scalar.activation(out=d[c][:, 2 * jp:2 * jp + 2, :], in_=b_banks[h, jp][:, :, lo:lo + CH], func=ACT.Abs)
+
+            def inverse_root(c, jp):
+                nc.scalar.activation(out=q_t[c][:, 2 * jp:2 * jp + 2, :], in_=d[c][:, 2 * jp:2 * jp + 2, :],
+                                     func=ACT.Abs_reciprocal_sqrt, bias=1.0)
+
+            magnitude(first, 0)
+            magnitude(second, 0)
+            magnitude(first, 1)
+            inverse_root(first, 0)
+            inverse_root(first, 1)
+            magnitude(second, 1)
+            inverse_root(second, 0)
+            inverse_root(second, 1)
 
         def factor(c):
             w = keep.tile([P, PACK, CH], F32, name="w", bufs=NCH)
@@ -194,6 +205,15 @@ def tile_mix_hidden_divided_hidden_kernel(
                 nc.vector.scalar_tensor_tensor(
                     out=w[:, j, :], in0=q_t[c][:, j, :], scalar=us_sb[:, j:j + 1], in1=q_t[c][:, j, :],
                     op0=ALU.mult, op1=ALU.mult)
+            w_t[c] = w
+
+        def factor_on_scalar(c):
+            qq = keep.tile([P, PACK, CH], F32, name="absb", bufs=2)
+            w = keep.tile([P, PACK, CH], F32, name="w", bufs=NCH)
+            for h in (slice(0, 2), slice(2, 4)):
+                nc.scalar.activation(out=qq[:, h, :], in_=q_t[c][:, h, :], func=ACT.Square)
+            for j in range(PACK):
+                nc.scalar.activation(out=w[:, j, :], in_=qq[:, j, :], func=ACT.Copy, scale=us_sb[:, j:j + 1])
             w_t[c] = w
 
         hid = sb("hid", [P, T * PACK], BF16)
@@ -223,9 +243,10 @@ def tile_mix_hidden_divided_hidden_kernel(
                 nc.scalar.copy(out=res[:], in_=o_banks[g, part][:])
             nc.sync.dma_start(out=out_v[:, a0:a1, t0:t0 + nt], in_=res[:])
 
-        for c in range(NCH):
-            mm_b(c)
-            root(c)
+        for h in range(2):
+            for jp in range(2):
+                mm_b(h, jp)
+            root(h)
         for c in range(NCH):
             mm_a(c)
         factor(0)
@@ -235,7 +256,7 @@ def tile_mix_hidden_divided_hidden_kernel(
         factor(2)
         quant(0)
         hidden(2)
-        factor(3)
+        factor_on_scalar(3)
         quant(1)
         hidden(3)
         quant(2)

from contextlib import ExitStack

import concourse.mybir as mybir

K, L, T, R, N = 1024, 512, 512, 512, 512
FLOPS = 2 * T * (K * R + L * R + R * N + K * N)

F32 = mybir.dt.float32
BF16 = mybir.dt.bfloat16
I32 = mybir.dt.int32
U32 = mybir.dt.uint32
U16 = mybir.dt.uint16
U8 = mybir.dt.uint8
FP8X4 = mybir.dt.float8_e4m3fn_x4
FP4X4 = mybir.dt.float4_e2m1fn_x4
ACT = mybir.ActivationFunctionType
ALU = mybir.AluOpType

P = 128
PACK = 4
CH = 128
NCH = T // CH


def tile_mix_hidden_divided_hidden_kernel(
    tc, xt_words, xt_scales, wa_words, wa_scales, xq_words, xq_scales, wc_words, wc_scales,
    us, wb_words, wb_scales, wy_words, wy_scales, out,
):
    nc = tc.nc
    with ExitStack() as ctx:
        keep = ctx.enter_context(tc.tile_pool(name="keep", bufs=1))
        psum = ctx.enter_context(tc.psum_pool(name="psum", bufs=1))
        ctx.enter_context(tc.manual_schedule())

        def sb(name, shape, dtype):
            return keep.tile(shape, dtype, name=name, align_bytes=64)

        xt_h = [sb("xt_w%d" % h, [P, 2, 256], U32) for h in range(2)]

        def xt_codes(z, t0, nt):
            return xt_h[t0 // 256][:, z, t0 % 256:t0 % 256 + nt].bitcast(FP8X4)

        xq_w = sb("xq_w", [P, 1, T], U32)
        wb_w = sb("wb_w", [P, 1, N], U32)
        wy_w = sb("wy_w", [P, 2, 2 * N], U8)
        wa_raw = sb("wa_raw", [P, 2, 2 * R], U8)
        wc_raw = sb("wc_raw", [P, 1, 2 * R], U8)
        wa_w = sb("wa_w", [P, PACK, 2, 2 * P], U8)
        wc_w = sb("wc_w", [P, PACK, 1, 2 * P], U8)
        wa_s = sb("wa_s", [P, PACK, 2, P], U8)
        wc_s = sb("wc_s", [P, PACK, 1, P], U8)
        wc_sraw = sb("wc_sraw", [P, R], U8)
        xq_s = sb("xq_s", [P, T], U8)
        wa_sraw = sb("wa_sraw", [P, 2 * R], U8)
        xt_s = sb("xt_s", [P, 2 * T], U8)
        wy_s = sb("wy_s", [P, 2 * N], U8)
        wb_s = sb("wb_s", [P, N], U8)
        us_sb = sb("us_sb", [P, PACK], F32)

        def load_e4m3(eng, tile, words):
            eng.dma_start(out=tile[:].bitcast(I32), in_=words.rearrange("z p c r -> p z (c r)").bitcast(I32))

        def load_e2m1(eng, tile, words):
            eng.dma_start(out=tile[:].bitcast(I32), in_=words.rearrange("z p c -> p z c").bitcast(I32))

        def load_scale_rows(eng, plane, scales, r):
            z = scales.shape[0]
            dst = plane[r:P:32, :].bitcast(I32).rearrange("q (z c) -> q z c", z=z)
            src = scales.rearrange("z (q r) c -> r q z c", r=4)[r].bitcast(I32)
            eng.dma_start(out=dst, in_=src)

        nc.gpsimd.memset(wc_sraw[:].bitcast(I32), 0)
        for plane in (xq_s, wa_sraw, xt_s, wy_s, wb_s):
            nc.vector.memset(plane[:].bitcast(I32), 0)

        xt_v = xt_words.rearrange("z p c r -> p z (c r)").bitcast(I32)

        for r in range(4):
            load_scale_rows(nc.sync, wc_sraw, wc_scales, r)
        load_e2m1(nc.sync, wc_raw, wc_words)
        load_e4m3(nc.sync, xq_w, xq_words)
        for r in range(4):
            load_scale_rows(nc.sync, xq_s, xq_scales, r)
        nc.gpsimd.dma_start(out=us_sb[:], in_=us.rearrange("(p j) o -> p (j o)", j=PACK))
        for r in range(2):
            load_scale_rows(nc.sync, wa_sraw, wa_scales, r)
        load_e2m1(nc.sync, wa_raw, wa_words)
        for r in range(2, 4):
            load_scale_rows(nc.sync, wa_sraw, wa_scales, r)
        nc.sync.dma_start(out=xt_h[0][:].bitcast(I32), in_=xt_v[:, :, 0:256])
        for r in range(4):
            load_scale_rows(nc.sync, xt_s, xt_scales, r)
        nc.sync.dma_start(out=xt_h[1][:].bitcast(I32), in_=xt_v[:, :, 256:512])
        load_e2m1(nc.sync, wy_w, wy_words)
        for r in range(4):
            load_scale_rows(nc.sync, wy_s, wy_scales, r)
        load_e4m3(nc.sync, wb_w, wb_words)
        for r in range(4):
            load_scale_rows(nc.sync, wb_s, wb_scales, r)

        warm = sb("warm", [P, 2], F32)
        nc.vector.memset(warm[:], 1.0)
        nc.scalar.activation(out=warm[:, 1:2], in_=warm[:, 0:1], func=ACT.Abs_reciprocal_sqrt)

        nc.scalar.copy(
            out=wc_w[:].rearrange("p j z b -> p j (z b)").bitcast(U16).rearrange("p j (g i) -> p g j i", i=8),
            in_=wc_raw[:].rearrange("p z b -> p (z b)").bitcast(U16).rearrange("p (g i j) -> p g j i", i=8, j=PACK),
        )
        nc.vector.tensor_copy(
            out=wc_s[:].rearrange("p j z (g i) -> p (z g) j i", i=16),
            in_=wc_sraw[:].rearrange("p (g i j) -> p g j i", i=16, j=PACK),
        )
        nc.vector.tensor_copy(
            out=wa_w[:].rearrange("p j z b -> p j (z b)").bitcast(U16).rearrange("p j (g i) -> p g j i", i=8),
            in_=wa_raw[:].rearrange("p z b -> p (z b)").bitcast(U16).rearrange("p (g i j) -> p g j i", i=8, j=PACK),
        )
        for h in (slice(0, 2), slice(2, 4)):
            nc.vector.tensor_copy(
                out=wa_s[:, h, :, :].rearrange("p j z (g i) -> p (z g) j i", i=16),
                in_=wa_sraw[:].rearrange("p (g i j) -> p g j i", i=16, j=PACK)[:, :, h, :],
            )

        b_banks, a_banks, o_banks = {}, {}, {}
        q_t, w_t, hq_w, hq_s = {}, {}, {}, {}

        def tok(c):
            return slice(c * CH, (c + 1) * CH)

        def mm_b(h, jp):
            bank = psum.tile([P, 2, 256], F32, name="b_bank", tag="bank%d" % (2 * h + jp))
            b_banks[h, jp] = bank
            for jj in range(2):
                j = 2 * jp + jj
                nc.tensor.matmul_mx(
                    out=bank[:, jj, :], lhsT=wc_w[:, j, 0, :].bitcast(FP4X4), lhsT_scale=wc_s[:, j, 0, :],
                    rhs=xq_w[:, 0, 256 * h:256 * (h + 1)].bitcast(FP8X4), rhs_scale=xq_s[:, 256 * h:256 * (h + 1)],
                    start=True, stop=True)

        def mm_a(c):
            bank = psum.tile([P, PACK, CH], F32, name="a_bank", tag="bank%d" % (NCH + c))
            a_banks[c] = bank
            for j in range(PACK):
                for z in range(2):
                    nc.tensor.matmul_mx(
                        out=bank[:, j, :], lhsT=wa_w[:, j, z, :].bitcast(FP4X4), lhsT_scale=wa_s[:, j, z, :],
                        rhs=xt_codes(z, c * CH, CH),
                        rhs_scale=xt_s[:, 512 * z + c * CH:512 * z + (c + 1) * CH], start=(z == 0), stop=(z == 1))

        groups = [
            (0, 256, [(0, 0, 2), (1, 2, 4)]),
            (256, 128, [(2, 0, 4)]),
            (384, 128, [(3, 0, 2), (4, 2, 4)]),
        ]

        def mm_y(g, part):
            t0, nt, parts = groups[g]
            tag, a0, a1 = parts[part]
            bank = psum.tile([P, a1 - a0, nt], F32, name="o_bank", tag="bank%d" % tag)
            o_banks[g, part] = bank
            for a in range(a0, a1):
                for z in range(2):
                    nc.tensor.matmul_mx(
                        out=bank[:, a - a0, :], lhsT=wy_w[:, z, 2 * P * a:2 * P * (a + 1)].bitcast(FP4X4),
                        lhsT_scale=wy_s[:, 512 * z + P * a:512 * z + P * (a + 1)],
                        rhs=xt_codes(z, t0, nt),
                        rhs_scale=xt_s[:, 512 * z + t0:512 * z + t0 + nt],
                        start=(a == a0 and z == 0), stop=False)

        def mm_o(g, part):
            t0, nt, parts = groups[g]
            tag, a0, a1 = parts[part]
            for a in range(a0, a1):
                nc.tensor.matmul_mx(
                    out=o_banks[g, part][:, a - a0, :], lhsT=wb_w[:, 0, P * a:P * (a + 1)].bitcast(FP8X4),
                    lhsT_scale=wb_s[:, P * a:P * (a + 1)],
                    rhs=hq_w[g][:].bitcast(FP8X4), rhs_scale=hq_s[g][:], start=False, stop=(a == a1 - 1))

        def root(h):
            first, second = 2 * h, 2 * h + 1
            d = {}
            for c in (first, second):
                d[c] = keep.tile([P, PACK, CH], F32, name="absb", bufs=2)
                q_t[c] = keep.tile([P, PACK, CH], F32, name="q", bufs=NCH)

            def magnitude(c, jp):
                lo = (c % 2) * CH
                nc.scalar.activation(out=d[c][:, 2 * jp:2 * jp + 2, :], in_=b_banks[h, jp][:, :, lo:lo + CH], func=ACT.Abs)

            def inverse_root(c, jp):
                nc.scalar.activation(out=q_t[c][:, 2 * jp:2 * jp + 2, :], in_=d[c][:, 2 * jp:2 * jp + 2, :],
                                     func=ACT.Abs_reciprocal_sqrt, bias=1.0)

            magnitude(first, 0)
            magnitude(second, 0)
            magnitude(first, 1)
            inverse_root(first, 0)
            inverse_root(first, 1)
            magnitude(second, 1)
            inverse_root(second, 0)
            inverse_root(second, 1)

        def factor(c):
            w = keep.tile([P, PACK, CH], F32, name="w", bufs=NCH)
            for j in range(PACK):
                nc.vector.scalar_tensor_tensor(
                    out=w[:, j, :], in0=q_t[c][:, j, :], scalar=us_sb[:, j:j + 1], in1=q_t[c][:, j, :],
                    op0=ALU.mult, op1=ALU.mult)
            w_t[c] = w

        def factor_on_scalar(c):
            qq = keep.tile([P, PACK, CH], F32, name="absb", bufs=2)
            w = keep.tile([P, PACK, CH], F32, name="w", bufs=NCH)
            for h in (slice(0, 2), slice(2, 4)):
                nc.scalar.activation(out=qq[:, h, :], in_=q_t[c][:, h, :], func=ACT.Square)
            for j in range(PACK):
                nc.scalar.activation(out=w[:, j, :], in_=qq[:, j, :], func=ACT.Copy, scale=us_sb[:, j:j + 1])
            w_t[c] = w

        hid = sb("hid", [P, T * PACK], BF16)

        def hidden(c):
            nc.vector.tensor_tensor(
                out=hid[:, c * CH * PACK:(c + 1) * CH * PACK].rearrange("p (g i j) -> p g j i", i=4, j=PACK),
                in0=a_banks[c][:].rearrange("p j (g i) -> p g j i", i=4),
                in1=w_t[c][:].rearrange("p j (g i) -> p g j i", i=4), op=ALU.mult)

        def quant(g):
            t0, nt, parts = groups[g]
            cw = sb("hq_w%d" % g, [P, nt], U32)
            cs = sb("hq_s%d" % g, [P, nt], U8)
            nc.vector.quantize_mx(out=cw[:].bitcast(FP8X4), scales=cs[:], in_=hid[:, t0 * PACK:(t0 + nt) * PACK])
            hq_w[g], hq_s[g] = cw, cs

        out_v = out.rearrange("(a p) t -> p a t", p=P)

        def drain(g, part, on_vector):
            t0, nt, parts = groups[g]
            tag, a0, a1 = parts[part]
            res = keep.tile([P, a1 - a0, nt], F32, name="res", bufs=5)
            if on_vector:
                nc.vector.tensor_copy(out=res[:], in_=o_banks[g, part][:])
            else:
                nc.scalar.copy(out=res[:], in_=o_banks[g, part][:])
            nc.sync.dma_start(out=out_v[:, a0:a1, t0:t0 + nt], in_=res[:])

        for h in range(2):
            for jp in range(2):
                mm_b(h, jp)
            root(h)
        for c in range(NCH):
            mm_a(c)
        factor(0)
        factor(1)
        hidden(0)
        hidden(1)
        factor(2)
        quant(0)
        hidden(2)
        factor_on_scalar(3)
        quant(1)
        hidden(3)
        quant(2)
        mm_y(0, 0)
        mm_y(0, 1)
        mm_o(0, 0)
        mm_o(0, 1)
        mm_y(1, 0)
        mm_o(1, 0)
        mm_y(2, 0)
        mm_y(2, 1)
        mm_o(2, 0)
        mm_o(2, 1)
        drain(0, 0, False)
        drain(0, 1, False)
        drain(1, 0, False)
        drain(2, 0, False)
        drain(2, 1, True)
